import numpy as np
import ml_dtypes


def mxq(x, axis, fmt="e4m3"):
    dtype, down = {"e4m3": (ml_dtypes.float8_e4m3fn, 7), "e5m2": (ml_dtypes.float8_e5m2, 14)}[fmt]
    v = np.moveaxis(np.asarray(x, np.float32).astype(ml_dtypes.bfloat16).astype(np.float64), axis, -1)
    blocks = v.reshape(v.shape[:-1] + (-1, 32))
    amax = np.abs(blocks).max(-1, keepdims=True)
    byte = np.maximum(np.where(amax > 0, np.frexp(amax)[1] - 1 + 127, 0) - down, 1)
    scale = np.exp2(byte - 127.0)
    codes = (blocks / scale).astype(np.float32).astype(dtype).astype(np.float64)
    return np.moveaxis((codes * scale).reshape(v.shape), -1, axis)


WIDE = False


def mx_kscale(k):
    if not WIDE:
        return np.ones(k)
    levels = np.array([10, -10, 5, -5, 0])
    if k % 512:
        return np.exp2(np.random.permutation(np.resize(levels, k // 32))).repeat(32)
    a = np.empty((k // 512, 16))
    for p in range(k // 512):
        a[p, :8] = np.random.permutation(np.resize(levels, 8))
        for g in range(8):
            far = levels[np.abs(levels - a[p, g]) >= 10]
            a[p, g + 8] = far[np.random.randint(len(far))]
    return np.exp2(a.ravel()).repeat(32)


def f64(x):
    return np.asarray(x).astype(np.float64)


def striped(idx):
    return np.tile(idx.reshape(-1, 16).T, (8, 1)).astype(np.uint16)


def unstriped(offs):
    return offs[:16].T.reshape(-1).astype(np.int64)


E2M1 = np.array([0.0, 0.5, 1.0, 1.5, 2.0, 3.0, 4.0, 6.0, -0.0, -0.5, -1.0, -1.5, -2.0, -3.0, -4.0, -6.0])


def pack_weight(w, fmt):
    k, n = w.shape
    w = f64(np.asarray(w, np.float32).astype(ml_dtypes.bfloat16)).reshape(k // 32, 32, n)
    amax = np.abs(w).max(1)
    if fmt == "e4m3":
        byte = np.frexp(amax)[1] - 1 + 127 - 7
    else:
        mant, ex = np.frexp(amax / 6.0)
        byte = np.where(mant > 0.5, ex, ex - 1) + 127
    byte = np.clip(np.where(amax > 0, byte, 1), 1, 254)
    scaled = (w * np.exp2(127.0 - byte)[:, None, :]).reshape(k, n).astype(np.float32)
    by_word = np.ascontiguousarray(scaled.reshape(k // 512, 128, 4, n).transpose(0, 1, 3, 2))
    if fmt == "e4m3":
        words = by_word.astype(ml_dtypes.float8_e4m3fn).view(np.uint8)
    else:
        c = by_word.astype(ml_dtypes.float4_e2m1fn).view(np.uint8) & 0xF
        words = (c[..., 0::2] | (c[..., 1::2] << 4)).reshape(k // 512, 128, 2 * n)
    return np.ascontiguousarray(words), np.ascontiguousarray(byte.astype(np.uint8).reshape(k // 512, 16, n))


def unpack_weight(words, scales, fmt):
    g, _, n = scales.shape
    words = np.ascontiguousarray(words).reshape(g, 128, n, -1)
    if fmt == "e4m3":
        vals = words.view(ml_dtypes.float8_e4m3fn).astype(np.float64)
    else:
        nib = np.empty((g, 128, n, 4), np.uint8)
        nib[..., 0::2] = words & 0xF
        nib[..., 1::2] = words >> 4
        vals = E2M1[nib]
    vals = vals * np.repeat(np.exp2(scales.astype(np.float64) - 127.0), 8, axis=1)[..., None]
    return vals.transpose(0, 1, 3, 2).reshape(g * 512, n)


def gelu(v):
    return 0.5 * v * (1.0 + np.tanh(np.sqrt(2.0 / np.pi) * (v + 0.044715 * v**3)))


K, T, S, H, T2, P = 1024, 2048, 512, 1536, 1024, 512


def setup_inputs():
    n = np.random.standard_normal
    s = mx_kscale(K)[:, None]
    u = mx_kscale(H)[:, None]
    d = {}
    d["tab_words"], d["tab_scales"] = pack_weight(n((K, T)) * s, "e4m3")
    d["offs"] = striped(np.random.permutation(T)[:S])
    d["w1"] = (n((K, H)) / K ** 0.5 / s * u.T).astype(np.float32)
    d["w4_words"], d["w4_scales"] = pack_weight(1.2 * n((K, H)) / K ** 0.5 / s * u.T, "e2m1")
    d["page0"] = (n((H, T2)) * u).astype(np.float32)
    d["wgs"] = np.exp(0.3 * n((128, S))).astype(np.float32)
    d["offs2"] = striped(np.random.permutation(T2)[:S])
    d["offs3"] = striped(np.random.permutation(T2)[:P])
    d["low"] = ((0.4 * n(H) - 0.6) * u[:, 0]).astype(np.float32)
    d["gain"] = (1.6 * n(H) / H ** 0.5 / u[:, 0] ** 2).astype(np.float32)
    d["slot"] = n(T2).astype(np.float32)
    return d


def reference(tab_words, tab_scales, offs, w1, w4_words, w4_scales, page0, wgs, offs2, offs3, low, gain, slot):
    v = unpack_weight(tab_words, tab_scales, "e4m3")[:, unstriped(offs)]
    a = mxq(f64(w1), 0, "e4m3").T @ v
    b = unpack_weight(w4_words, w4_scales, "e2m1").T @ v
    h = a - np.abs(b)
    page = f64(page0).copy()
    page[:, unstriped(offs2)] = np.tile(f64(wgs), (H // 128, 1)) * h
    x = page[:, unstriped(offs3)]
    x = np.maximum(x, f64(low)[:, None]) * f64(gain)[:, None]
    e = mxq(page, 0, "e4m3").T @ mxq(x, 0, "e4m3")
    return 1.0 / (1.0 + np.exp(-(e + f64(slot)[:, None])))

@@ -1,0 +1,355 @@
+from contextlib import ExitStack
+
+import concourse.mybir as mybir
+from concourse.masks import make_identity
+
+K, T, S, H, T2, NX = 1024, 2048, 512, 1536, 1024, 512
+FLOPS = 2 * (2 * K * H * S + H * T2 * NX)
+
+F32 = mybir.dt.float32
+BF16 = mybir.dt.bfloat16
+I32 = mybir.dt.int32
+U32 = mybir.dt.uint32
+U16 = mybir.dt.uint16
+U8 = mybir.dt.uint8
+FP8X4 = mybir.dt.float8_e4m3fn_x4
+FP4X4 = mybir.dt.float4_e2m1fn_x4
+ACT = mybir.ActivationFunctionType
+ALU = mybir.AluOpType
+
+P = 128
+PACK = 4
+PASS = P * PACK
+K_PASSES = K // PASS
+R_PASSES = H // PASS
+J_TILES = S // P
+M_TILES = T2 // P
+LAST = R_PASSES - 1
+RUN = 4
+
+
+def woven(ap):
+    return ap.rearrange("p (c i) t -> p c t i", i=RUN)
+
+
+def planar(ap):
+    return ap.rearrange("p t (c i) -> p c t i", i=RUN)
+
+
+def tile_list_hydrant_survey_board_kernel(
+    tc, tab_words, tab_scales, offs, w1, w4_words, w4_scales, page0, wgs, offs2, offs3, low, gain, slot, out
+):
+    nc = tc.nc
+    with ExitStack() as ctx:
+        lists = ctx.enter_context(tc.tile_pool(name="lists", bufs=1))
+        sb = ctx.enter_context(tc.tile_pool(name="sb", bufs=1))
+        psum = ctx.enter_context(tc.psum_pool(name="psum", bufs=1))
+
+        def sbuf(shape, dtype, name, tag=None, bufs=1):
+            return sb.tile(shape, dtype, name=name, tag=tag or name, bufs=bufs, align_bytes=64)
+
+        def bank(number, name):
+            return psum.tile([P, PASS], F32, name=name, tag="bank%d" % number)
+
+        idx = lists.tile([P, S // 16], U16, name="idx")
+        idx2 = lists.tile([P, S // 16], U16, name="idx2")
+        idx3 = lists.tile([P, NX // 16], U16, name="idx3")
+
+        tab_s = sbuf([P, K_PASSES, T], U8, "tab_s", tag="x_last")
+        w4_s = sbuf([P, K_PASSES, H], U8, "w4_s")
+        nc.gpsimd.memset(tab_s[:].bitcast(I32), 0)
+
+        def load_scale_rows(queue, plane, rows):
+            by_row = rows.rearrange("a q c -> q a c").bitcast(I32)
+            for quad in range(4):
+                queue.dma_start(out=plane[32 * quad : 32 * quad + 4].bitcast(I32), in_=by_row[4 * quad : 4 * quad + 4])
+
+        tab_w = [sbuf([P, T], U32, "tab_w%d" % a, tag=("neg_a1", "abs_b1")[a]) for a in range(K_PASSES)]
+
+        def load_tab(a):
+            nc.sync.dma_start(out=tab_w[a][:].bitcast(I32), in_=tab_words[a].rearrange("p t i -> p (t i)").bitcast(I32))
+
+        w1_raw = {}
+
+        def load_w1(b, a):
+            w1_raw[b, a] = sbuf([P, PACK, PASS], F32, "w1_raw%d%d" % (b, a), tag="w1_raw%d%d" % (b % 2, a))
+            rows = w1[a * PASS : (a + 1) * PASS, b * PASS : (b + 1) * PASS]
+            nc.sync.dma_start(out=w1_raw[b, a][:], in_=rows.rearrange("(p i) c -> p i c", i=PACK))
+
+        w4_w = {}
+
+        def load_w4(b):
+            w4_w[b] = sbuf([P, K_PASSES, 2 * PASS], U8, "w4_w%d" % b)
+            cols = w4_words.rearrange("a p c -> p a c")[:, :, 2 * PASS * b : 2 * PASS * (b + 1)]
+            nc.sync.dma_start(out=w4_w[b][:].bitcast(I32), in_=cols.bitcast(I32))
+
+        page = {}
+
+        def load_page(b, t):
+            page[b, t] = sbuf([P, T2], F32, "page%d%d" % (b, t), tag="page", bufs=8)
+            rows = page0[b * PASS : (b + 1) * PASS].rearrange("(p t) m -> t p m", t=PACK)
+            nc.sync.dma_start(out=page[b, t][:], in_=rows[t])
+
+        wgs_sb = [sbuf([P, 2, S], F32, "wgs_sb%d" % u) for u in range(2)]
+        wgs_rows = wgs.rearrange("(q t) j -> q t j", t=PACK)
+
+        def load_wgs(u):
+            for quad in range(4):
+                nc.sync.dma_start(out=wgs_sb[u][32 * quad : 32 * quad + 32], in_=wgs_rows[:, 2 * u : 2 * u + 2, :])
+
+        low_sb = sbuf([P, R_PASSES, PACK], F32, "low_sb")
+        gain_sb = sbuf([P, R_PASSES, PACK], F32, "gain_sb")
+        slot_sb = sbuf([P, M_TILES], F32, "slot_sb")
+        ident = sbuf([P, P], F32, "ident")
+
+        nc.sync.dma_start(idx[:], offs)
+        load_scale_rows(nc.sync, tab_s, tab_scales)
+        load_scale_rows(nc.sync, w4_s, w4_scales)
+        nc.sync.dma_start(idx2[:], offs2)
+        make_identity(nc, ident[:])
+        load_tab(0)
+        load_tab(1)
+        load_w4(0)
+        load_w1(0, 0)
+        load_w1(0, 1)
+        load_wgs(0)
+        load_page(0, 0)
+        load_page(0, 1)
+        nc.sync.dma_start(idx3[:], offs3)
+        nc.sync.dma_start(out=low_sb[:], in_=low.rearrange("(b p t) -> p b t", p=P, t=PACK))
+        nc.sync.dma_start(out=gain_sb[:], in_=gain.rearrange("(b p t) -> p b t", p=P, t=PACK))
+        load_w1(1, 0)
+        load_w1(1, 1)
+        load_w4(1)
+        load_wgs(1)
+        load_page(0, 2)
+        load_page(0, 3)
+
+        v_w = [sbuf([P, S], U32, "v_w%d" % a) for a in range(K_PASSES)]
+        v_s = [sbuf([P, S], U8, "v_s%d" % a) for a in range(K_PASSES)]
+        for a in range(K_PASSES):
+            nc.vector.tensor_copy(v_w[a][:], tab_w[a][:].indirect(idx[:]))
+            nc.vector.tensor_copy(v_s[a][:], tab_s[:, a, :].indirect(idx[:]))
+
+        w1_w, w1_s = {}, {}
+
+        def quantise_w1(b, a, vector_cols):
+            rounded = sbuf([P, PASS, PACK], BF16, "w1_bf%d%d" % (b, a), tag=(("x_last", "w1_bf1"), ("neg_a0", "abs_b0"), ("w1_bf0", "w1_bf1"))[b][a])
+            if vector_cols > 0:
+                nc.vector.tensor_copy(out=woven(rounded[:, :vector_cols, :]), in_=planar(w1_raw[b, a][:, :, :vector_cols]))
+            if vector_cols < PASS:
+                nc.scalar.copy(out=woven(rounded[:, vector_cols:, :]), in_=planar(w1_raw[b, a][:, :, vector_cols:]))
+            w1_w[b, a] = sbuf([P, PASS], U32, "w1_w%d%d" % (b, a))
+            w1_s[b, a] = sbuf([P, PASS], U8, "w1_s%d%d" % (b, a))
+            nc.vector.quantize_mx(
+                out=w1_w[b, a][:].bitcast(FP8X4), scales=w1_s[b, a][:], in_=rounded[:].rearrange("p c t -> p (c t)")
+            )
+
+        h = {}
+
+        def dealt(ap):
+            return ap.rearrange("j (p t) -> j t p", t=PACK)
+
+        def by_slice(ap):
+            return ap.rearrange("j (t p) -> j t p", t=PACK)
+
+        neg_a, abs_b, neg_h = {}, {}, {}
+
+        def sums_b(b):
+            abs_b[b] = sbuf([P, J_TILES, PASS], F32, "abs_b_%d" % b, tag="abs_b%d" % (b % 2))
+            cols = slice(b * PASS, (b + 1) * PASS)
+            for jt in range(J_TILES):
+                js = slice(jt * P, (jt + 1) * P)
+                acc = bank(4 + jt, "b_sum%d%d" % (b, jt))
+                for a in range(K_PASSES):
+                    nc.tensor.matmul_mx(
+                        out=acc[:],
+                        lhsT=v_w[a][:, js].bitcast(FP8X4),
+                        lhsT_scale=v_s[a][:, js],
+                        rhs=w4_w[b][:, a, :].bitcast(FP4X4),
+                        rhs_scale=w4_s[:, a, cols],
+                        start=(a == 0),
+                        stop=(a == K_PASSES - 1),
+                    )
+                nc.scalar.activation(out=by_slice(abs_b[b][:, jt, :]), in_=dealt(acc[:]), func=ACT.Abs)
+
+        def sums_a(b):
+            neg_a[b] = sbuf([P, J_TILES, PASS], F32, "neg_a_%d" % b, tag=("neg_a0", "neg_a1", "planes_hi0")[b])
+            sums = [bank(jt, "a_sum%d%d" % (b, jt)) for jt in range(J_TILES)]
+            for a in range(K_PASSES):
+                for jt in range(J_TILES):
+                    js = slice(jt * P, (jt + 1) * P)
+                    nc.tensor.matmul_mx(
+                        out=sums[jt][:],
+                        lhsT=v_w[a][:, js].bitcast(FP8X4),
+                        lhsT_scale=v_s[a][:, js],
+                        rhs=w1_w[b, a][:].bitcast(FP8X4),
+                        rhs_scale=w1_s[b, a][:],
+                        start=(a == 0),
+                        stop=(a == K_PASSES - 1),
+                    )
+            for jt in range(J_TILES):
+                dst = by_slice(neg_a[b][:, jt, :])
+                if b == 0 and jt % 2 == 1:
+                    nc.vector.tensor_scalar(out=dst, in0=dealt(sums[jt][:]), scalar1=-1.0, scalar2=None, op0=ALU.mult)
+                else:
+                    nc.scalar.activation(out=dst, in_=dealt(sums[jt][:]), func=ACT.Copy, scale=-1.0)
+
+        def turn(b, u):
+            for t in (2 * u, 2 * u + 1):
+                neg_h[b, t] = bank(t, "neg_h%d%d" % (b, t))
+                rs = slice(t * P, (t + 1) * P)
+                for jt in range(J_TILES):
+                    dst = neg_h[b, t][:, jt * P : (jt + 1) * P]
+                    nc.tensor.matmul(dst, abs_b[b][:, jt, rs], ident[:], is_transpose=True, start=True, stop=False)
+                    nc.tensor.matmul(dst, neg_a[b][:, jt, rs], ident[:], is_transpose=True, start=False, stop=True)
+
+        def take_h(b, u):
+            tag = (("h0", "w1_raw11"), ("w1_raw01", "h1"), ("h0", "planes_hi1"))[b][u]
+            h[b, u] = sbuf([P, 2, S], F32, "h%d%d" % (b, u), tag=tag)
+            for i in range(2):
+                nc.scalar.activation(out=h[b, u][:, i, :], in_=neg_h[b, 2 * u + i][:], func=ACT.Copy, scale=-1.0)
+
+        x_planes, page_planes, page_bf, x_bf = {}, {}, {}, {}
+
+        def change_and_pick(b, u):
+            direct = (b, u) == (LAST, 1)
+            picked = [sbuf([P, NX], F32, "picked%d%d%d" % (b, u, i), tag="picked", bufs=4) for i in range(2)]
+            if not direct:
+                x_planes[b, u] = sbuf([P, 2, NX], BF16, "x_planes%d%d" % (b, u), tag="x_planes", bufs=4)
+            for i in range(2):
+                t = 2 * u + i
+                nc.vector.tensor_tensor(page[b, t][:].indirect(idx2[:]), h[b, u][:, i, :], wgs_sb[u][:, i, :], ALU.mult)
+            for i in range(2):
+                nc.vector.tensor_copy(picked[i][:], page[b, 2 * u + i][:].indirect(idx3[:]))
+            for i in range(2):
+                t = 2 * u + i
+                nc.vector.tensor_scalar(
+                    out=x_bf[b][:, :, t] if direct else x_planes[b, u][:, i, :],
+                    in0=picked[i][:],
+                    scalar1=low_sb[:, b, t : t + 1],
+                    scalar2=gain_sb[:, b, t : t + 1],
+                    op0=ALU.max,
+                    op1=ALU.mult,
+                )
+
+        def collect(b, u):
+            tag = "planes_lo%d" % (b % 2) if u == 0 else "planes_hi%d" % b
+            page_planes[b, u] = sbuf([P, 2, T2], F32, "page_planes%d%d" % (b, u), tag=tag)
+            for i in range(2):
+                nc.sync.dma_start(out=page_planes[b, u][:, i, :], in_=page[b, 2 * u + i][:])
+            if b + 2 < R_PASSES:
+                for i in range(2):
+                    load_page(b + 2, 2 * u + i)
+
+        def weave(b, u):
+            if u == 0:
+                x_bf[b] = sbuf([P, NX, PACK], BF16, "x_bf%d" % b, tag=("abs_b1", "abs_b0", "x_last")[b])
+                page_bf[b] = sbuf([P, T2, PACK], BF16, "page_bf%d" % b, tag=("neg_a1", "planes_hi0", "neg_a0")[b])
+            ts = slice(2 * u, 2 * u + 2)
+            for m0 in range(0, T2, T2 // 2):
+                ms = slice(m0, m0 + T2 // 2)
+                nc.scalar.copy(out=woven(page_bf[b][:, ms, ts]), in_=planar(page_planes[b, u][:, :, ms]))
+            nc.scalar.copy(out=woven(x_bf[b][:, :, ts]), in_=planar(x_planes[b, u][:]))
+
+        page_w = [sbuf([P, T2], U32, "page_w%d" % b) for b in range(R_PASSES)]
+        page_s = [sbuf([P, T2], U8, "page_s%d" % b) for b in range(R_PASSES)]
+        x_w = [sbuf([P, NX], U32, "x_w%d" % b) for b in range(R_PASSES)]
+        x_s = [sbuf([P, NX], U8, "x_s%d" % b) for b in range(R_PASSES)]
+        CHUNK = 256
+
+        def quantise_x(b):
+            nc.vector.quantize_mx(out=x_w[b][:].bitcast(FP8X4), scales=x_s[b][:], in_=x_bf[b][:].rearrange("p c t -> p (c t)"))
+
+        def quantise_page(b, ms):
+            nc.vector.quantize_mx(
+                out=page_w[b][:, ms].bitcast(FP8X4), scales=page_s[b][:, ms], in_=page_bf[b][:, ms, :].rearrange("p c t -> p (c t)")
+            )
+
+        def second_operands(b):
+            for m0 in range(0, T2, 2 * CHUNK):
+                quantise_page(b, slice(m0, m0 + 2 * CHUNK))
+            quantise_x(b)
+
+        e = {}
+
+        def second_pass(b, mt):
+            ms = slice(mt * P, (mt + 1) * P)
+            nc.tensor.matmul_mx(
+                out=e[mt][:],
+                lhsT=page_w[b][:, ms].bitcast(FP8X4),
+                lhsT_scale=page_s[b][:, ms],
+                rhs=x_w[b][:].bitcast(FP8X4),
+                rhs_scale=x_s[b][:],
+                start=(b == LAST - 1),
+                stop=(b == LAST),
+            )
+
+        quantise_w1(0, 0, PASS)
+        quantise_w1(0, 1, 384)
+        load_w1(2, 0)
+        load_w1(2, 1)
+        for t in range(PACK):
+            load_page(1, t)
+        load_w4(2)
+        with nc.allow_non_contiguous_dma(reason="one value of slot to a partition"):
+            nc.sync.dma_start(out=slot_sb[:], in_=slot.rearrange("(c p) -> p c", p=P))
+
+        sums_b(0)
+        sums_a(0)
+        turn(0, 0)
+        take_h(0, 0)
+        turn(0, 1)
+        change_and_pick(0, 0)
+        collect(0, 0)
+        quantise_w1(1, 0, 0)
+        quantise_w1(1, 1, 0)
+        take_h(0, 1)
+        sums_b(1)
+        sums_a(1)
+        turn(1, 0)
+        change_and_pick(0, 1)
+        collect(0, 1)
+        quantise_w1(2, 0, 0)
+        quantise_w1(2, 1, 0)
+        take_h(1, 0)
+        turn(1, 1)
+        take_h(1, 1)
+        change_and_pick(1, 0)
+        collect(1, 0)
+        weave(0, 0)
+        sums_b(2)
+        change_and_pick(1, 1)
+        collect(1, 1)
+        weave(0, 1)
+        second_operands(0)
+        sums_a(2)
+        turn(2, 0)
+        take_h(2, 0)
+        turn(2, 1)
+        weave(1, 0)
+        change_and_pick(2, 0)
+        collect(2, 0)
+        weave(1, 1)
+        second_operands(1)
+        take_h(2, 1)
+
+        for mt in range(M_TILES):
+            e[mt] = bank(mt, "e%d" % mt)
+        for b in reversed(range(LAST)):
+            for mt in range(M_TILES):
+                second_pass(b, mt)
+        weave(LAST, 0)
+        change_and_pick(LAST, 1)
+        nc.scalar.copy(out=page_bf[LAST][:, :, 2], in_=page[LAST, 2][:])
+        quantise_x(LAST)
+        for m0 in range(0, T2, CHUNK):
+            ms = slice(m0, m0 + CHUNK)
+            nc.scalar.copy(out=page_bf[LAST][:, ms, PACK - 1], in_=page[LAST, PACK - 1][:, ms])
+            quantise_page(LAST, ms)
+        scores = [sbuf([P, M_TILES // 2, NX], F32, "scores%d" % i, tag=("w1_raw00", "w1_raw10")[i]) for i in range(2)]
+        for mt in range(M_TILES):
+            second_pass(LAST, mt)
+            score = scores[mt // 4][:, mt % 4, :]
+            nc.scalar.activation(out=score, in_=e[mt][:], func=ACT.Sigmoid, bias=slot_sb[:, mt : mt + 1])
+            nc.sync.dma_start(out=out[mt * P : (mt + 1) * P, :], in_=score)

@@ -56,7 +56,8 @@ def tile_list_hydrant_survey_board_kernel(
         idx3 = lists.tile([P, NX // 16], U16, name="idx3")
 
         tab_s = sbuf([P, K_PASSES, T], U8, "tab_s", tag="x_last")
-        w4_s = sbuf([P, K_PASSES, H], U8, "w4_s")
+        w4_s_first = sbuf([P, K_PASSES, PASS], U8, "w4_s_first")
+        w4_s_rest = sbuf([P, K_PASSES, H - PASS], U8, "w4_s_rest")
         nc.gpsimd.memset(tab_s[:].bitcast(I32), 0)
 
         def load_scale_rows(queue, plane, rows):
@@ -64,17 +65,19 @@ def tile_list_hydrant_survey_board_kernel(
             for quad in range(4):
                 queue.dma_start(out=plane[32 * quad : 32 * quad + 4].bitcast(I32), in_=by_row[4 * quad : 4 * quad + 4])
 
-        tab_w = [sbuf([P, T], U32, "tab_w%d" % a, tag=("neg_a1", "abs_b1")[a]) for a in range(K_PASSES)]
+        tab_w = [sbuf([P, T], U32, "tab_w%d" % a, tag=("tab_w0", "abs_b1")[a]) for a in range(K_PASSES)]
 
         def load_tab(a):
             nc.sync.dma_start(out=tab_w[a][:].bitcast(I32), in_=tab_words[a].rearrange("p t i -> p (t i)").bitcast(I32))
 
         w1_raw = {}
 
-        def load_w1(b, a):
+        def load_w1(b, a, pieces=1):
             w1_raw[b, a] = sbuf([P, PACK, PASS], F32, "w1_raw%d%d" % (b, a), tag="w1_raw%d%d" % (b % 2, a))
-            rows = w1[a * PASS : (a + 1) * PASS, b * PASS : (b + 1) * PASS]
-            nc.sync.dma_start(out=w1_raw[b, a][:], in_=rows.rearrange("(p i) c -> p i c", i=PACK))
+            rows = w1[a * PASS : (a + 1) * PASS, b * PASS : (b + 1) * PASS].rearrange("(p i) c -> p i c", i=PACK)
+            for c0 in range(0, PASS, PASS // pieces):
+                cs = slice(c0, c0 + PASS // pieces)
+                nc.sync.dma_start(out=w1_raw[b, a][:, :, cs], in_=rows[:, :, cs])
 
         w4_w = {}
 
@@ -94,7 +97,7 @@ def tile_list_hydrant_survey_board_kernel(
         wgs_rows = wgs.rearrange("(q t) j -> q t j", t=PACK)
 
         def load_wgs(u):
-            for quad in range(4):
+            for quad in (0, 2, 1, 3):
                 nc.sync.dma_start(out=wgs_sb[u][32 * quad : 32 * quad + 32], in_=wgs_rows[:, 2 * u : 2 * u + 2, :])
 
         low_sb = sbuf([P, R_PASSES, PACK], F32, "low_sb")
@@ -103,24 +106,25 @@ def tile_list_hydrant_survey_board_kernel(
         ident = sbuf([P, P], F32, "ident")
 
         nc.sync.dma_start(idx[:], offs)
-        load_scale_rows(nc.sync, tab_s, tab_scales)
-        load_scale_rows(nc.sync, w4_s, w4_scales)
+        load_scale_rows(nc.sync, w4_s_first, w4_scales[:, :, :PASS])
         nc.sync.dma_start(idx2[:], offs2)
-        make_identity(nc, ident[:])
+        nc.sync.dma_start(idx3[:], offs3)
         load_tab(0)
-        load_tab(1)
+        load_scale_rows(nc.sync, tab_s, tab_scales)
+        make_identity(nc, ident[:])
         load_w4(0)
+        load_tab(1)
         load_w1(0, 0)
-        load_w1(0, 1)
+        load_w1(0, 1, 2)
         load_wgs(0)
         load_page(0, 0)
         load_page(0, 1)
-        nc.sync.dma_start(idx3[:], offs3)
         nc.sync.dma_start(out=low_sb[:], in_=low.rearrange("(b p t) -> p b t", p=P, t=PACK))
         nc.sync.dma_start(out=gain_sb[:], in_=gain.rearrange("(b p t) -> p b t", p=P, t=PACK))
         load_w1(1, 0)
         load_w1(1, 1)
         load_w4(1)
+        load_scale_rows(nc.sync, w4_s_rest, w4_scales[:, :, PASS:])
         load_wgs(1)
         load_page(0, 2)
         load_page(0, 3)
@@ -133,17 +137,22 @@ def tile_list_hydrant_survey_board_kernel(
 
         w1_w, w1_s = {}, {}
 
-        def quantise_w1(b, a, vector_cols):
-            rounded = sbuf([P, PASS, PACK], BF16, "w1_bf%d%d" % (b, a), tag=(("x_last", "w1_bf1"), ("neg_a0", "abs_b0"), ("w1_bf0", "w1_bf1"))[b][a])
-            if vector_cols > 0:
-                nc.vector.tensor_copy(out=woven(rounded[:, :vector_cols, :]), in_=planar(w1_raw[b, a][:, :, :vector_cols]))
-            if vector_cols < PASS:
-                nc.scalar.copy(out=woven(rounded[:, vector_cols:, :]), in_=planar(w1_raw[b, a][:, :, vector_cols:]))
+        def quantise_w1(b, a, on_vector=False, pieces=1):
+            tag = (("x_last", "w1_bf1"), ("neg_a0", "abs_b0"), ("tab_w0", "w1_bf1"))[b][a]
+            rounded = sbuf([P, PASS, PACK], BF16, "w1_bf%d%d" % (b, a), tag=tag)
             w1_w[b, a] = sbuf([P, PASS], U32, "w1_w%d%d" % (b, a))
             w1_s[b, a] = sbuf([P, PASS], U8, "w1_s%d%d" % (b, a))
-            nc.vector.quantize_mx(
-                out=w1_w[b, a][:].bitcast(FP8X4), scales=w1_s[b, a][:], in_=rounded[:].rearrange("p c t -> p (c t)")
-            )
+            for c0 in range(0, PASS, PASS // pieces):
+                cs = slice(c0, c0 + PASS // pieces)
+                copy = nc.vector.tensor_copy if on_vector else nc.scalar.copy
+                copy(out=woven(rounded[:, cs, :]), in_=planar(w1_raw[b, a][:, :, cs]))
+            for c0 in range(0, PASS, PASS // pieces):
+                cs = slice(c0, c0 + PASS // pieces)
+                nc.vector.quantize_mx(
+                    out=w1_w[b, a][:, cs].bitcast(FP8X4),
+                    scales=w1_s[b, a][:, cs],
+                    in_=rounded[:, cs, :].rearrange("p c t -> p (c t)"),
+                )
 
         h = {}
 
@@ -157,7 +166,7 @@ def tile_list_hydrant_survey_board_kernel(
 
         def sums_b(b):
             abs_b[b] = sbuf([P, J_TILES, PASS], F32, "abs_b_%d" % b, tag="abs_b%d" % (b % 2))
-            cols = slice(b * PASS, (b + 1) * PASS)
+            scales = w4_s_first if b == 0 else w4_s_rest[:, :, (b - 1) * PASS : b * PASS]
             for jt in range(J_TILES):
                 js = slice(jt * P, (jt + 1) * P)
                 acc = bank(4 + jt, "b_sum%d%d" % (b, jt))
@@ -167,26 +176,28 @@ def tile_list_hydrant_survey_board_kernel(
                         lhsT=v_w[a][:, js].bitcast(FP8X4),
                         lhsT_scale=v_s[a][:, js],
                         rhs=w4_w[b][:, a, :].bitcast(FP4X4),
-                        rhs_scale=w4_s[:, a, cols],
+                        rhs_scale=scales[:, a, :],
                         start=(a == 0),
                         stop=(a == K_PASSES - 1),
                     )
                 nc.scalar.activation(out=by_slice(abs_b[b][:, jt, :]), in_=dealt(acc[:]), func=ACT.Abs)
 
-        def sums_a(b):
-            neg_a[b] = sbuf([P, J_TILES, PASS], F32, "neg_a_%d" % b, tag=("neg_a0", "neg_a1", "planes_hi0")[b])
+        def sums_a(b, pieces=1):
+            neg_a[b] = sbuf([P, J_TILES, PASS], F32, "neg_a_%d" % b, tag=("neg_a0", "w1_raw00", "planes0")[b])
             sums = [bank(jt, "a_sum%d%d" % (b, jt)) for jt in range(J_TILES)]
-            for a in range(K_PASSES):
+            passes = [(0, slice(0, PASS))]
+            passes.extend((1, slice(c0, c0 + PASS // pieces)) for c0 in range(0, PASS, PASS // pieces))
+            for n, (a, cs) in enumerate(passes):
                 for jt in range(J_TILES):
                     js = slice(jt * P, (jt + 1) * P)
                     nc.tensor.matmul_mx(
-                        out=sums[jt][:],
+                        out=sums[jt][:, cs],
                         lhsT=v_w[a][:, js].bitcast(FP8X4),
                         lhsT_scale=v_s[a][:, js],
-                        rhs=w1_w[b, a][:].bitcast(FP8X4),
-                        rhs_scale=w1_s[b, a][:],
-                        start=(a == 0),
-                        stop=(a == K_PASSES - 1),
+                        rhs=w1_w[b, a][:, cs].bitcast(FP8X4),
+                        rhs_scale=w1_s[b, a][:, cs],
+                        start=(n == 0),
+                        stop=(n == len(passes) - 1),
                     )
             for jt in range(J_TILES):
                 dst = by_slice(neg_a[b][:, jt, :])
@@ -197,35 +208,40 @@ def tile_list_hydrant_survey_board_kernel(
 
         def turn(b, u):
             for t in (2 * u, 2 * u + 1):
-                neg_h[b, t] = bank(t, "neg_h%d%d" % (b, t))
+                neg_h[b, t] = bank((t + 4) % 6 if b == 0 else t, "neg_h%d%d" % (b, t))
                 rs = slice(t * P, (t + 1) * P)
-                for jt in range(J_TILES):
+                terms = [(term, jt) for term in (abs_b[b], neg_a[b]) for jt in range(J_TILES)]
+                for n, (term, jt) in enumerate(terms):
                     dst = neg_h[b, t][:, jt * P : (jt + 1) * P]
-                    nc.tensor.matmul(dst, abs_b[b][:, jt, rs], ident[:], is_transpose=True, start=True, stop=False)
-                    nc.tensor.matmul(dst, neg_a[b][:, jt, rs], ident[:], is_transpose=True, start=False, stop=True)
+                    nc.tensor.matmul(
+                        dst, term[:, jt, rs], ident[:], is_transpose=True, start=(n == 0), stop=(n == len(terms) - 1)
+                    )
 
-        def take_h(b, u):
-            tag = (("h0", "w1_raw11"), ("w1_raw01", "h1"), ("h0", "planes_hi1"))[b][u]
-            h[b, u] = sbuf([P, 2, S], F32, "h%d%d" % (b, u), tag=tag)
-            for i in range(2):
-                nc.scalar.activation(out=h[b, u][:, i, :], in_=neg_h[b, 2 * u + i][:], func=ACT.Copy, scale=-1.0)
+        def take_h(b, ts, tag):
+            held = sbuf([P, len(ts), S], F32, "h%d%d" % (b, ts[0]), tag=tag)
+            for i, t in enumerate(ts):
+                h[b, t] = held[:, i, :]
+                nc.scalar.activation(out=h[b, t], in_=neg_h[b, t][:], func=ACT.Copy, scale=-1.0)
 
         x_planes, page_planes, page_bf, x_bf = {}, {}, {}, {}
+
+        def planes_of(b):
+            return 2 if b == LAST else PACK
 
         def change_and_pick(b, u):
             direct = (b, u) == (LAST, 1)
             picked = [sbuf([P, NX], F32, "picked%d%d%d" % (b, u, i), tag="picked", bufs=4) for i in range(2)]
-            if not direct:
-                x_planes[b, u] = sbuf([P, 2, NX], BF16, "x_planes%d%d" % (b, u), tag="x_planes", bufs=4)
+            if u == 0:
+                x_planes[b] = sbuf([P, planes_of(b), NX], BF16, "x_planes%d" % b, tag="x_planes", bufs=2)
             for i in range(2):
                 t = 2 * u + i
-                nc.vector.tensor_tensor(page[b, t][:].indirect(idx2[:]), h[b, u][:, i, :], wgs_sb[u][:, i, :], ALU.mult)
+                nc.vector.tensor_tensor(page[b, t][:].indirect(idx2[:]), h[b, t], wgs_sb[u][:, i, :], ALU.mult)
             for i in range(2):
                 nc.vector.tensor_copy(picked[i][:], page[b, 2 * u + i][:].indirect(idx3[:]))
             for i in range(2):
                 t = 2 * u + i
                 nc.vector.tensor_scalar(
-                    out=x_bf[b][:, :, t] if direct else x_planes[b, u][:, i, :],
+                    out=x_bf[b][:, :, t] if direct else x_planes[b][:, t, :],
                     in0=picked[i][:],
                     scalar1=low_sb[:, b, t : t + 1],
                     scalar2=gain_sb[:, b, t : t + 1],
@@ -234,23 +250,28 @@ def tile_list_hydrant_survey_board_kernel(
                 )
 
         def collect(b, u):
-            tag = "planes_lo%d" % (b % 2) if u == 0 else "planes_hi%d" % b
-            page_planes[b, u] = sbuf([P, 2, T2], F32, "page_planes%d%d" % (b, u), tag=tag)
-            for i in range(2):
-                nc.sync.dma_start(out=page_planes[b, u][:, i, :], in_=page[b, 2 * u + i][:])
+            if u == 0:
+                tag = ("planes0", "planes1", "w1_raw10")[b]
+                page_planes[b] = sbuf([P, planes_of(b), T2], F32, "page_planes%d" % b, tag=tag)
+            for t in (2 * u, 2 * u + 1):
+                nc.sync.dma_start(out=page_planes[b][:, t, :], in_=page[b, t][:])
             if b + 2 < R_PASSES:
                 for i in range(2):
                     load_page(b + 2, 2 * u + i)
 
-        def weave(b, u):
-            if u == 0:
-                x_bf[b] = sbuf([P, NX, PACK], BF16, "x_bf%d" % b, tag=("abs_b1", "abs_b0", "x_last")[b])
-                page_bf[b] = sbuf([P, T2, PACK], BF16, "page_bf%d" % b, tag=("neg_a1", "planes_hi0", "neg_a0")[b])
-            ts = slice(2 * u, 2 * u + 2)
-            for m0 in range(0, T2, T2 // 2):
-                ms = slice(m0, m0 + T2 // 2)
-                nc.scalar.copy(out=woven(page_bf[b][:, ms, ts]), in_=planar(page_planes[b, u][:, :, ms]))
-            nc.scalar.copy(out=woven(x_bf[b][:, :, ts]), in_=planar(x_planes[b, u][:]))
+        def weave(b):
+            both = sbuf([P, T2 + NX, PACK], BF16, "second_bf%d" % b, tag=("w1_raw00", "planes0", "neg_a0")[b])
+            page_bf[b], x_bf[b] = both[:, :T2, :], both[:, T2:, :]
+            if b == LAST:
+                for m0 in range(0, T2, T2 // 2):
+                    ms = slice(m0, m0 + T2 // 2)
+                    nc.scalar.copy(out=page_bf[b][:, ms, :2], in_=page_planes[b][:, :, ms].rearrange("p t c -> p c t"))
+                nc.scalar.copy(out=x_bf[b][:, :, :2], in_=x_planes[b][:].rearrange("p t c -> p c t"))
+            else:
+                for m0 in range(0, T2, T2 // 2):
+                    ms = slice(m0, m0 + T2 // 2)
+                    nc.scalar.copy(out=woven(page_bf[b][:, ms, :]), in_=planar(page_planes[b][:, :, ms]))
+                nc.scalar.copy(out=woven(x_bf[b]), in_=planar(x_planes[b][:]))
 
         page_w = [sbuf([P, T2], U32, "page_w%d" % b) for b in range(R_PASSES)]
         page_s = [sbuf([P, T2], U8, "page_s%d" % b) for b in range(R_PASSES)]
@@ -259,7 +280,7 @@ def tile_list_hydrant_survey_board_kernel(
         CHUNK = 256
 
         def quantise_x(b):
-            nc.vector.quantize_mx(out=x_w[b][:].bitcast(FP8X4), scales=x_s[b][:], in_=x_bf[b][:].rearrange("p c t -> p (c t)"))
+            nc.vector.quantize_mx(out=x_w[b][:].bitcast(FP8X4), scales=x_s[b][:], in_=x_bf[b].rearrange("p c t -> p (c t)"))
 
         def quantise_page(b, ms):
             nc.vector.quantize_mx(
@@ -285,8 +306,8 @@ def tile_list_hydrant_survey_board_kernel(
                 stop=(b == LAST),
             )
 
-        quantise_w1(0, 0, PASS)
-        quantise_w1(0, 1, 384)
+        quantise_w1(0, 0, True)
+        quantise_w1(0, 1, True, 2)
         load_w1(2, 0)
         load_w1(2, 1)
         for t in range(PACK):
@@ -296,50 +317,47 @@ def tile_list_hydrant_survey_board_kernel(
             nc.sync.dma_start(out=slot_sb[:], in_=slot.rearrange("(c p) -> p c", p=P))
 
         sums_b(0)
-        sums_a(0)
+        sums_a(0, 2)
         turn(0, 0)
-        take_h(0, 0)
+        take_h(0, (0, 1), "h0")
         turn(0, 1)
         change_and_pick(0, 0)
         collect(0, 0)
-        quantise_w1(1, 0, 0)
-        quantise_w1(1, 1, 0)
-        take_h(0, 1)
+        quantise_w1(1, 0)
+        quantise_w1(1, 1)
+        take_h(0, (2, 3), "w1_raw11")
         sums_b(1)
+        quantise_w1(2, 0)
         sums_a(1)
         turn(1, 0)
+        turn(1, 1)
         change_and_pick(0, 1)
         collect(0, 1)
-        quantise_w1(2, 0, 0)
-        quantise_w1(2, 1, 0)
-        take_h(1, 0)
-        turn(1, 1)
-        take_h(1, 1)
+        quantise_w1(2, 1)
+        take_h(1, (0, 1, 2, 3), "w1_raw01")
         change_and_pick(1, 0)
         collect(1, 0)
-        weave(0, 0)
         sums_b(2)
         change_and_pick(1, 1)
         collect(1, 1)
-        weave(0, 1)
+        weave(0)
         second_operands(0)
         sums_a(2)
         turn(2, 0)
-        take_h(2, 0)
+        take_h(2, (0, 1), "h0")
         turn(2, 1)
-        weave(1, 0)
         change_and_pick(2, 0)
         collect(2, 0)
-        weave(1, 1)
+        weave(1)
         second_operands(1)
-        take_h(2, 1)
+        take_h(2, (2, 3), "planes1")
 
         for mt in range(M_TILES):
             e[mt] = bank(mt, "e%d" % mt)
         for b in reversed(range(LAST)):
             for mt in range(M_TILES):
                 second_pass(b, mt)
-        weave(LAST, 0)
+        weave(LAST)
         change_and_pick(LAST, 1)
         nc.scalar.copy(out=page_bf[LAST][:, :, 2], in_=page[LAST, 2][:])
         quantise_x(LAST)

from contextlib import ExitStack

import concourse.mybir as mybir
from concourse.masks import make_identity

K, T, S, H, T2, NX = 1024, 2048, 512, 1536, 1024, 512
FLOPS = 2 * (2 * K * H * S + H * T2 * NX)

F32 = mybir.dt.float32
BF16 = mybir.dt.bfloat16
I32 = mybir.dt.int32
U32 = mybir.dt.uint32
U16 = mybir.dt.uint16
U8 = mybir.dt.uint8
FP8X4 = mybir.dt.float8_e4m3fn_x4
FP4X4 = mybir.dt.float4_e2m1fn_x4
ACT = mybir.ActivationFunctionType
ALU = mybir.AluOpType

P = 128
PACK = 4
PASS = P * PACK
K_PASSES = K // PASS
R_PASSES = H // PASS
J_TILES = S // P
M_TILES = T2 // P
LAST = R_PASSES - 1
RUN = 4


def woven(ap):
    return ap.rearrange("p (c i) t -> p c t i", i=RUN)


def planar(ap):
    return ap.rearrange("p t (c i) -> p c t i", i=RUN)


def tile_list_hydrant_survey_board_kernel(
    tc, tab_words, tab_scales, offs, w1, w4_words, w4_scales, page0, wgs, offs2, offs3, low, gain, slot, out
):
    nc = tc.nc
    with ExitStack() as ctx:
        lists = ctx.enter_context(tc.tile_pool(name="lists", bufs=1))
        sb = ctx.enter_context(tc.tile_pool(name="sb", bufs=1))
        psum = ctx.enter_context(tc.psum_pool(name="psum", bufs=1))

        def sbuf(shape, dtype, name, tag=None, bufs=1):
            return sb.tile(shape, dtype, name=name, tag=tag or name, bufs=bufs, align_bytes=64)

        def bank(number, name):
            return psum.tile([P, PASS], F32, name=name, tag="bank%d" % number)

        idx = lists.tile([P, S // 16], U16, name="idx")
        idx2 = lists.tile([P, S // 16], U16, name="idx2")
        idx3 = lists.tile([P, NX // 16], U16, name="idx3")

        tab_s = sbuf([P, K_PASSES, T], U8, "tab_s", tag="x_last")
        w4_s_first = sbuf([P, K_PASSES, PASS], U8, "w4_s_first")
        w4_s_rest = sbuf([P, K_PASSES, H - PASS], U8, "w4_s_rest")
        nc.gpsimd.memset(tab_s[:].bitcast(I32), 0)

        def load_scale_rows(queue, plane, rows):
            by_row = rows.rearrange("a q c -> q a c").bitcast(I32)
            for quad in range(4):
                queue.dma_start(out=plane[32 * quad : 32 * quad + 4].bitcast(I32), in_=by_row[4 * quad : 4 * quad + 4])

        tab_w = [sbuf([P, T], U32, "tab_w%d" % a, tag=("tab_w0", "abs_b1")[a]) for a in range(K_PASSES)]

        def load_tab(a):
            nc.sync.dma_start(out=tab_w[a][:].bitcast(I32), in_=tab_words[a].rearrange("p t i -> p (t i)").bitcast(I32))

        w1_raw = {}

        def load_w1(b, a, pieces=1):
            w1_raw[b, a] = sbuf([P, PACK, PASS], F32, "w1_raw%d%d" % (b, a), tag="w1_raw%d%d" % (b % 2, a))
            rows = w1[a * PASS : (a + 1) * PASS, b * PASS : (b + 1) * PASS].rearrange("(p i) c -> p i c", i=PACK)
            for c0 in range(0, PASS, PASS // pieces):
                cs = slice(c0, c0 + PASS // pieces)
                nc.sync.dma_start(out=w1_raw[b, a][:, :, cs], in_=rows[:, :, cs])

        w4_w = {}

        def load_w4(b):
            w4_w[b] = sbuf([P, K_PASSES, 2 * PASS], U8, "w4_w%d" % b)
            cols = w4_words.rearrange("a p c -> p a c")[:, :, 2 * PASS * b : 2 * PASS * (b + 1)]
            nc.sync.dma_start(out=w4_w[b][:].bitcast(I32), in_=cols.bitcast(I32))

        page = {}

        def load_page(b, t):
            page[b, t] = sbuf([P, T2], F32, "page%d%d" % (b, t), tag="page", bufs=8)
            rows = page0[b * PASS : (b + 1) * PASS].rearrange("(p t) m -> t p m", t=PACK)
            nc.sync.dma_start(out=page[b, t][:], in_=rows[t])

        wgs_sb = [sbuf([P, 2, S], F32, "wgs_sb%d" % u) for u in range(2)]
        wgs_rows = wgs.rearrange("(q t) j -> q t j", t=PACK)

        def load_wgs(u):
            for quad in (0, 2, 1, 3):
                nc.sync.dma_start(out=wgs_sb[u][32 * quad : 32 * quad + 32], in_=wgs_rows[:, 2 * u : 2 * u + 2, :])

        low_sb = sbuf([P, R_PASSES, PACK], F32, "low_sb")
        gain_sb = sbuf([P, R_PASSES, PACK], F32, "gain_sb")
        slot_sb = sbuf([P, M_TILES], F32, "slot_sb")
        ident = sbuf([P, P], F32, "ident")

        nc.sync.dma_start(idx[:], offs)
        load_scale_rows(nc.sync, w4_s_first, w4_scales[:, :, :PASS])
        nc.sync.dma_start(idx2[:], offs2)
        nc.sync.dma_start(idx3[:], offs3)
        load_tab(0)
        load_scale_rows(nc.sync, tab_s, tab_scales)
        make_identity(nc, ident[:])
        load_w4(0)
        load_tab(1)
        load_w1(0, 0)
        load_w1(0, 1, 2)
        load_wgs(0)
        load_page(0, 0)
        load_page(0, 1)
        nc.sync.dma_start(out=low_sb[:], in_=low.rearrange("(b p t) -> p b t", p=P, t=PACK))
        nc.sync.dma_start(out=gain_sb[:], in_=gain.rearrange("(b p t) -> p b t", p=P, t=PACK))
        load_w1(1, 0)
        load_w1(1, 1)
        load_w4(1)
        load_scale_rows(nc.sync, w4_s_rest, w4_scales[:, :, PASS:])
        load_wgs(1)
        load_page(0, 2)
        load_page(0, 3)

        v_w = [sbuf([P, S], U32, "v_w%d" % a) for a in range(K_PASSES)]
        v_s = [sbuf([P, S], U8, "v_s%d" % a) for a in range(K_PASSES)]
        for a in range(K_PASSES):
            nc.vector.tensor_copy(v_w[a][:], tab_w[a][:].indirect(idx[:]))
            nc.vector.tensor_copy(v_s[a][:], tab_s[:, a, :].indirect(idx[:]))

        w1_w, w1_s = {}, {}

        def quantise_w1(b, a, on_vector=False, pieces=1):
            tag = (("x_last", "w1_bf1"), ("neg_a0", "abs_b0"), ("tab_w0", "w1_bf1"))[b][a]
            rounded = sbuf([P, PASS, PACK], BF16, "w1_bf%d%d" % (b, a), tag=tag)
            w1_w[b, a] = sbuf([P, PASS], U32, "w1_w%d%d" % (b, a))
            w1_s[b, a] = sbuf([P, PASS], U8, "w1_s%d%d" % (b, a))
            for c0 in range(0, PASS, PASS // pieces):
                cs = slice(c0, c0 + PASS // pieces)
                copy = nc.vector.tensor_copy if on_vector else nc.scalar.copy
                copy(out=woven(rounded[:, cs, :]), in_=planar(w1_raw[b, a][:, :, cs]))
            for c0 in range(0, PASS, PASS // pieces):
                cs = slice(c0, c0 + PASS // pieces)
                nc.vector.quantize_mx(
                    out=w1_w[b, a][:, cs].bitcast(FP8X4),
                    scales=w1_s[b, a][:, cs],
                    in_=rounded[:, cs, :].rearrange("p c t -> p (c t)"),
                )

        h = {}

        def dealt(ap):
            return ap.rearrange("j (p t) -> j t p", t=PACK)

        def by_slice(ap):
            return ap.rearrange("j (t p) -> j t p", t=PACK)

        neg_a, abs_b, neg_h = {}, {}, {}

        def sums_b(b):
            abs_b[b] = sbuf([P, J_TILES, PASS], F32, "abs_b_%d" % b, tag="abs_b%d" % (b % 2))
            scales = w4_s_first if b == 0 else w4_s_rest[:, :, (b - 1) * PASS : b * PASS]
            for jt in range(J_TILES):
                js = slice(jt * P, (jt + 1) * P)
                acc = bank(4 + jt, "b_sum%d%d" % (b, jt))
                for a in range(K_PASSES):
                    nc.tensor.matmul_mx(
                        out=acc[:],
                        lhsT=v_w[a][:, js].bitcast(FP8X4),
                        lhsT_scale=v_s[a][:, js],
                        rhs=w4_w[b][:, a, :].bitcast(FP4X4),
                        rhs_scale=scales[:, a, :],
                        start=(a == 0),
                        stop=(a == K_PASSES - 1),
                    )
                nc.scalar.activation(out=by_slice(abs_b[b][:, jt, :]), in_=dealt(acc[:]), func=ACT.Abs)

        def sums_a(b, pieces=1):
            neg_a[b] = sbuf([P, J_TILES, PASS], F32, "neg_a_%d" % b, tag=("neg_a0", "w1_raw00", "planes0")[b])
            sums = [bank(jt, "a_sum%d%d" % (b, jt)) for jt in range(J_TILES)]
            passes = [(0, slice(0, PASS))]
            passes.extend((1, slice(c0, c0 + PASS // pieces)) for c0 in range(0, PASS, PASS // pieces))
            for n, (a, cs) in enumerate(passes):
                for jt in range(J_TILES):
                    js = slice(jt * P, (jt + 1) * P)
                    nc.tensor.matmul_mx(
                        out=sums[jt][:, cs],
                        lhsT=v_w[a][:, js].bitcast(FP8X4),
                        lhsT_scale=v_s[a][:, js],
                        rhs=w1_w[b, a][:, cs].bitcast(FP8X4),
                        rhs_scale=w1_s[b, a][:, cs],
                        start=(n == 0),
                        stop=(n == len(passes) - 1),
                    )
            for jt in range(J_TILES):
                dst = by_slice(neg_a[b][:, jt, :])
                if b == 0 and jt % 2 == 1:
                    nc.vector.tensor_scalar(out=dst, in0=dealt(sums[jt][:]), scalar1=-1.0, scalar2=None, op0=ALU.mult)
                else:
                    nc.scalar.activation(out=dst, in_=dealt(sums[jt][:]), func=ACT.Copy, scale=-1.0)

        def turn(b, u):
            for t in (2 * u, 2 * u + 1):
                neg_h[b, t] = bank((t + 4) % 6 if b == 0 else t, "neg_h%d%d" % (b, t))
                rs = slice(t * P, (t + 1) * P)
                terms = [(term, jt) for term in (abs_b[b], neg_a[b]) for jt in range(J_TILES)]
                for n, (term, jt) in enumerate(terms):
                    dst = neg_h[b, t][:, jt * P : (jt + 1) * P]
                    nc.tensor.matmul(
                        dst, term[:, jt, rs], ident[:], is_transpose=True, start=(n == 0), stop=(n == len(terms) - 1)
                    )

        def take_h(b, ts, tag):
            held = sbuf([P, len(ts), S], F32, "h%d%d" % (b, ts[0]), tag=tag)
            for i, t in enumerate(ts):
                h[b, t] = held[:, i, :]
                nc.scalar.activation(out=h[b, t], in_=neg_h[b, t][:], func=ACT.Copy, scale=-1.0)

        x_planes, page_planes, page_bf, x_bf = {}, {}, {}, {}

        def planes_of(b):
            return 2 if b == LAST else PACK

        def change_and_pick(b, u):
            direct = (b, u) == (LAST, 1)
            picked = [sbuf([P, NX], F32, "picked%d%d%d" % (b, u, i), tag="picked", bufs=4) for i in range(2)]
            if u == 0:
                x_planes[b] = sbuf([P, planes_of(b), NX], BF16, "x_planes%d" % b, tag="x_planes", bufs=2)
            for i in range(2):
                t = 2 * u + i
                nc.vector.tensor_tensor(page[b, t][:].indirect(idx2[:]), h[b, t], wgs_sb[u][:, i, :], ALU.mult)
            for i in range(2):
                nc.vector.tensor_copy(picked[i][:], page[b, 2 * u + i][:].indirect(idx3[:]))
            for i in range(2):
                t = 2 * u + i
                nc.vector.tensor_scalar(
                    out=x_bf[b][:, :, t] if direct else x_planes[b][:, t, :],
                    in0=picked[i][:],
                    scalar1=low_sb[:, b, t : t + 1],
                    scalar2=gain_sb[:, b, t : t + 1],
                    op0=ALU.max,
                    op1=ALU.mult,
                )

        def collect(b, u):
            if u == 0:
                tag = ("planes0", "planes1", "w1_raw10")[b]
                page_planes[b] = sbuf([P, planes_of(b), T2], F32, "page_planes%d" % b, tag=tag)
            for t in (2 * u, 2 * u + 1):
                nc.sync.dma_start(out=page_planes[b][:, t, :], in_=page[b, t][:])
            if b + 2 < R_PASSES:
                for i in range(2):
                    load_page(b + 2, 2 * u + i)

        def weave(b):
            both = sbuf([P, T2 + NX, PACK], BF16, "second_bf%d" % b, tag=("w1_raw00", "planes0", "neg_a0")[b])
            page_bf[b], x_bf[b] = both[:, :T2, :], both[:, T2:, :]
            if b == LAST:
                for m0 in range(0, T2, T2 // 2):
                    ms = slice(m0, m0 + T2 // 2)
                    nc.scalar.copy(out=page_bf[b][:, ms, :2], in_=page_planes[b][:, :, ms].rearrange("p t c -> p c t"))
                nc.scalar.copy(out=x_bf[b][:, :, :2], in_=x_planes[b][:].rearrange("p t c -> p c t"))
            else:
                for m0 in range(0, T2, T2 // 2):
                    ms = slice(m0, m0 + T2 // 2)
                    nc.scalar.copy(out=woven(page_bf[b][:, ms, :]), in_=planar(page_planes[b][:, :, ms]))
                nc.scalar.copy(out=woven(x_bf[b]), in_=planar(x_planes[b][:]))

        page_w = [sbuf([P, T2], U32, "page_w%d" % b) for b in range(R_PASSES)]
        page_s = [sbuf([P, T2], U8, "page_s%d" % b) for b in range(R_PASSES)]
        x_w = [sbuf([P, NX], U32, "x_w%d" % b) for b in range(R_PASSES)]
        x_s = [sbuf([P, NX], U8, "x_s%d" % b) for b in range(R_PASSES)]
        CHUNK = 256

        def quantise_x(b):
            nc.vector.quantize_mx(out=x_w[b][:].bitcast(FP8X4), scales=x_s[b][:], in_=x_bf[b].rearrange("p c t -> p (c t)"))

        def quantise_page(b, ms):
            nc.vector.quantize_mx(
                out=page_w[b][:, ms].bitcast(FP8X4), scales=page_s[b][:, ms], in_=page_bf[b][:, ms, :].rearrange("p c t -> p (c t)")
            )

        def second_operands(b):
            for m0 in range(0, T2, 2 * CHUNK):
                quantise_page(b, slice(m0, m0 + 2 * CHUNK))
            quantise_x(b)

        e = {}

        def second_pass(b, mt):
            ms = slice(mt * P, (mt + 1) * P)
            nc.tensor.matmul_mx(
                out=e[mt][:],
                lhsT=page_w[b][:, ms].bitcast(FP8X4),
                lhsT_scale=page_s[b][:, ms],
                rhs=x_w[b][:].bitcast(FP8X4),
                rhs_scale=x_s[b][:],
                start=(b == LAST - 1),
                stop=(b == LAST),
            )

        quantise_w1(0, 0, True)
        quantise_w1(0, 1, True, 2)
        load_w1(2, 0)
        load_w1(2, 1)
        for t in range(PACK):
            load_page(1, t)
        load_w4(2)
        with nc.allow_non_contiguous_dma(reason="one value of slot to a partition"):
            nc.sync.dma_start(out=slot_sb[:], in_=slot.rearrange("(c p) -> p c", p=P))

        sums_b(0)
        sums_a(0, 2)
        turn(0, 0)
        take_h(0, (0, 1), "h0")
        turn(0, 1)
        change_and_pick(0, 0)
        collect(0, 0)
        quantise_w1(1, 0)
        quantise_w1(1, 1)
        take_h(0, (2, 3), "w1_raw11")
        sums_b(1)
        quantise_w1(2, 0)
        sums_a(1)
        turn(1, 0)
        turn(1, 1)
        change_and_pick(0, 1)
        collect(0, 1)
        quantise_w1(2, 1)
        take_h(1, (0, 1, 2, 3), "w1_raw01")
        change_and_pick(1, 0)
        collect(1, 0)
        sums_b(2)
        change_and_pick(1, 1)
        collect(1, 1)
        weave(0)
        second_operands(0)
        sums_a(2)
        turn(2, 0)
        take_h(2, (0, 1), "h0")
        turn(2, 1)
        change_and_pick(2, 0)
        collect(2, 0)
        weave(1)
        second_operands(1)
        take_h(2, (2, 3), "planes1")

        for mt in range(M_TILES):
            e[mt] = bank(mt, "e%d" % mt)
        for b in reversed(range(LAST)):
            for mt in range(M_TILES):
                second_pass(b, mt)
        weave(LAST)
        change_and_pick(LAST, 1)
        nc.scalar.copy(out=page_bf[LAST][:, :, 2], in_=page[LAST, 2][:])
        quantise_x(LAST)
        for m0 in range(0, T2, CHUNK):
            ms = slice(m0, m0 + CHUNK)
            nc.scalar.copy(out=page_bf[LAST][:, ms, PACK - 1], in_=page[LAST, PACK - 1][:, ms])
            quantise_page(LAST, ms)
        scores = [sbuf([P, M_TILES // 2, NX], F32, "scores%d" % i, tag=("w1_raw00", "w1_raw10")[i]) for i in range(2)]
        for mt in range(M_TILES):
            second_pass(LAST, mt)
            score = scores[mt // 4][:, mt % 4, :]
            nc.scalar.activation(out=score, in_=e[mt][:], func=ACT.Sigmoid, bias=slot_sb[:, mt : mt + 1])
            nc.sync.dma_start(out=out[mt * P : (mt + 1) * P, :], in_=score)
